import numpy as np
import ml_dtypes


def mxq(x, axis, fmt="e4m3"):
    dtype, down = {"e4m3": (ml_dtypes.float8_e4m3fn, 7), "e5m2": (ml_dtypes.float8_e5m2, 14)}[fmt]
    v = np.moveaxis(np.asarray(x, np.float32).astype(ml_dtypes.bfloat16).astype(np.float64), axis, -1)
    blocks = v.reshape(v.shape[:-1] + (-1, 32))
    amax = np.abs(blocks).max(-1, keepdims=True)
    byte = np.maximum(np.where(amax > 0, np.frexp(amax)[1] - 1 + 127, 0) - down, 1)
    scale = np.exp2(byte - 127.0)
    codes = (blocks / scale).astype(np.float32).astype(dtype).astype(np.float64)
    return np.moveaxis((codes * scale).reshape(v.shape), -1, axis)


WIDE = False


def mx_kscale(k):
    if not WIDE:
        return np.ones(k)
    levels = np.array([10, -10, 5, -5, 0])
    if k % 512:
        return np.exp2(np.random.permutation(np.resize(levels, k // 32))).repeat(32)
    a = np.empty((k // 512, 16))
    for p in range(k // 512):
        a[p, :8] = np.random.permutation(np.resize(levels, 8))
        for g in range(8):
            far = levels[np.abs(levels - a[p, g]) >= 10]
            a[p, g + 8] = far[np.random.randint(len(far))]
    return np.exp2(a.ravel()).repeat(32)


def f64(x):
    return np.asarray(x).astype(np.float64)


def striped(idx):
    return np.tile(idx.reshape(-1, 16).T, (8, 1)).astype(np.uint16)


def unstriped(offs):
    return offs[:16].T.reshape(-1).astype(np.int64)


def striped8(idx):
    return np.concatenate([x.reshape(-1, 16).T for x in idx]).astype(np.uint16)


def runs(offs, k):
    lists = np.stack([offs[16 * r : 16 * r + 16].T.reshape(-1) for r in range(8)]).astype(np.int64)
    return lists[np.arange(k) % 512 // 64]


def pack_weight(w):
    k, n = w.shape
    w = f64(np.asarray(w, np.float32).astype(ml_dtypes.bfloat16)).reshape(k // 32, 32, n)
    amax = np.abs(w).max(1)
    byte = np.clip(np.where(amax > 0, np.frexp(amax)[1] - 1 + 127 - 7, 1), 1, 254)
    scaled = (w * np.exp2(127.0 - byte)[:, None, :]).reshape(k, n).astype(np.float32)
    words = np.ascontiguousarray(scaled.reshape(k // 512, 128, 4, n).transpose(0, 1, 3, 2)).astype(ml_dtypes.float8_e4m3fn).view(np.uint8)
    return words, np.ascontiguousarray(byte.astype(np.uint8).reshape(k // 512, 16, n))


def unpack_weight(words, scales):
    g, p, n, _ = words.shape
    vals = np.ascontiguousarray(words).view(ml_dtypes.float8_e4m3fn).astype(np.float64) * np.repeat(np.exp2(scales.astype(np.float64) - 127.0), 8, axis=1)[..., None]
    return vals.transpose(0, 1, 3, 2).reshape(g * 512, n)


E2M1 = np.array([0.0, 0.5, 1.0, 1.5, 2.0, 3.0, 4.0, 6.0, -0.0, -0.5, -1.0, -1.5, -2.0, -3.0, -4.0, -6.0])


def pack_fp4(w):
    k, n = w.shape
    w = f64(np.asarray(w, np.float32).astype(ml_dtypes.bfloat16)).reshape(k // 32, 32, n)
    amax = np.abs(w).max(1)
    mant, ex = np.frexp(amax / 6.0)
    byte = np.clip(np.where(amax > 0, np.where(mant > 0.5, ex, ex - 1) + 127, 1), 1, 254)
    scaled = (w * np.exp2(127.0 - byte)[:, None, :]).reshape(k, n).astype(np.float32)
    c = np.ascontiguousarray(scaled.reshape(k // 512, 128, 4, n).transpose(0, 1, 3, 2)).astype(ml_dtypes.float4_e2m1fn).view(np.uint8) & 0xF
    words = (c[..., 0::2] | (c[..., 1::2] << 4)).reshape(k // 512, 128, 2 * n)
    return np.ascontiguousarray(words), np.ascontiguousarray(byte.astype(np.uint8).reshape(k // 512, 16, n))


def unpack_fp4(words, scales):
    g, _, n = scales.shape
    words = np.ascontiguousarray(words).reshape(g, 128, n, 2)
    nib = np.empty((g, 128, n, 4), np.uint8)
    nib[..., 0::2] = words & 0xF
    nib[..., 1::2] = words >> 4
    vals = E2M1[nib] * np.repeat(np.exp2(scales.astype(np.float64) - 127.0), 8, axis=1)[..., None]
    return vals.transpose(0, 1, 3, 2).reshape(g * 512, n)


K, T, S, N, G, H, W = 512, 1024, 256, 512, 2048, 512, 128


def setup_inputs():
    n = np.random.standard_normal
    s = mx_kscale(K)[:, None]
    u = mx_kscale(K)
    packed_xT = pack_weight(n((K, T)) * s)
    packed_dT = pack_weight(n((K, G)) / s)
    packed_w1 = pack_fp4(n((H, N)) / np.sqrt(H) / u[:, None])
    perm = np.random.permutation(S)
    return {
        "x_words": packed_xT[0],
        "x_scales": packed_xT[1],
        "d_words": packed_dT[0],
        "d_scales": packed_dT[1],
        "gn": (np.random.uniform(0.5, 1.5, (H, 1)) * u[:, None]).astype(np.float32),
        "w1_words": packed_w1[0],
        "w1_scales": packed_w1[1],
        "offs": striped(np.random.permutation(T)[:S]),
        "k1": striped8(np.random.randint(0, G, (8, H))),
        "two": striped(np.random.permutation(T)[:S]),
        "k2": striped8(np.random.randint(0, G, (8, H))),
        "hz": striped8(np.random.randint(0, T, (8, S))),
        "k3": striped8(np.random.randint(0, G, (8, H))),
        "n1": striped(np.random.permutation(S)),
        "n2": striped(np.random.permutation(S)),
        "n3": striped(perm[:W]),
        "n4": striped(perm[W:]),
    }


def reference(x_words, x_scales, d_words, d_scales, gn, w1_words, w1_scales, offs, k1, two, k2, hz, k3, n1, n2, n3, n4):
    d_k1 = unpack_weight(d_words, d_scales)[np.arange(K)[:, None], runs(k1, K)]
    xq = unpack_weight(x_words, x_scales)[:, unstriped(offs)]
    d_k2 = unpack_weight(d_words, d_scales)[np.arange(K)[:, None], runs(k2, K)]
    x_two = unpack_weight(x_words, x_scales)[:, unstriped(two)]
    d_k3 = unpack_weight(d_words, d_scales)[np.arange(K)[:, None], runs(k3, K)]
    x_hz = unpack_weight(x_words, x_scales)[np.arange(K)[:, None], runs(hz, K)]
    h = 0.0625 * (d_k1.T @ xq + d_k2.T @ x_two + d_k3.T @ x_hz)
    ds = np.zeros((H, S))
    ds[:, unstriped(n1)] = h
    ds2 = np.zeros((H, S))
    ds2[:, unstriped(n2)] = h
    z = f64(gn) * (ds - ds2)
    h2 = unpack_fp4(w1_words, w1_scales).T @ mxq(z, 0, "e4m3")
    pa = h2[:, unstriped(n3)]
    pb = h2[:, unstriped(n4)]
    rb = pa - pb
    ra = 0.75 * (pa + pb)
    ua = np.zeros((N, S))
    ua[:, unstriped(n3)] = ra
    out = ua.copy()
    out[:, unstriped(n4)] = rb
    return out

@@ -1,0 +1,215 @@
+from contextlib import ExitStack
+
+import concourse.mybir as mybir
+from concourse.masks import make_identity
+
+K, T, S, N, G, H, W = 512, 1024, 256, 512, 2048, 512, 128
+FLOPS = 2 * K * H * S * 3 + 2 * H * N * S
+
+F32 = mybir.dt.float32
+BF16 = mybir.dt.bfloat16
+I32 = mybir.dt.int32
+U32 = mybir.dt.uint32
+U16 = mybir.dt.uint16
+U8 = mybir.dt.uint8
+FP8X4 = mybir.dt.float8_e4m3fn_x4
+FP4X4 = mybir.dt.float4_e2m1fn_x4
+COPY = mybir.ActivationFunctionType.Copy
+ALU = mybir.AluOpType
+
+P = 128
+HALF = H // 2
+SPARE = 2 * S
+
+
+def tile_picked_mtthznsndsubhaar_none_p_kernel(
+    tc, x_words, x_scales, d_words, d_scales, gn, w1_words, w1_scales, offs, k1, two, k2, hz, k3, n1, n2, n3, n4, out
+):
+    nc = tc.nc
+    with ExitStack() as ctx:
+        keep = ctx.enter_context(tc.tile_pool(name="keep", bufs=1))
+        psum = ctx.enter_context(tc.psum_pool(name="psum", bufs=1))
+
+        def load_list(name, src):
+            t = keep.tile(list(src.shape), U16, name=name)
+            nc.sync.dma_start(t[:], src)
+            return t
+
+        d_sc = keep.tile([P, G], U8, name="d_sc", align_bytes=64)
+        x_sc = keep.tile([P, T], U8, name="x_sc", align_bytes=64)
+        plane0 = keep.tile([P, 3 * HALF + 3 * S], U8, name="plane0", align_bytes=64)
+        plane1 = keep.tile([P, 3 * HALF], U8, name="plane1", align_bytes=64)
+        w_sc = keep.tile([P, N], U8, name="w_sc", align_bytes=64)
+        nc.vector.memset(w_sc[:].bitcast(I32), 0)
+        nc.vector.memset(plane0[:].bitcast(I32), 0)
+        nc.vector.memset(plane1[:].bitcast(I32), 0)
+
+        d_w = keep.tile([P, G], I32, name="d_w", align_bytes=64)
+        x_w = keep.tile([P, T], I32, name="x_w", align_bytes=64)
+        l_k1 = load_list("l_k1", k1)
+        nc.sync.dma_start(d_sc[:].bitcast(I32), d_scales[0].bitcast(I32).unsqueeze(1).to_broadcast([16, 8, G // 4]))
+        l_k2 = load_list("l_k2", k2)
+        l_k3 = load_list("l_k3", k3)
+        nc.sync.dma_start(x_sc[:].bitcast(I32), x_scales[0].bitcast(I32).unsqueeze(1).to_broadcast([16, 8, T // 4]))
+        l_offs = load_list("l_offs", offs)
+        l_two = load_list("l_two", two)
+        l_hz = load_list("l_hz", hz)
+        nc.sync.dma_start(d_w[:], d_words[0].rearrange("p n t -> p (n t)").bitcast(I32))
+        nc.sync.dma_start(x_w[:], x_words[0].rearrange("p n t -> p (n t)").bitcast(I32))
+        l_n1 = load_list("l_n1", n1)
+        l_n2 = load_list("l_n2", n2)
+        l_n3 = load_list("l_n3", n3)
+        l_n4 = load_list("l_n4", n4)
+        d_lists = [l_k1, l_k2, l_k3]
+        x_lists = [l_offs, l_two, l_hz]
+
+        gain = keep.tile([P, 4], F32, name="gain")
+        with nc.allow_non_contiguous_dma(reason="one gain a partition"):
+            nc.gpsimd.dma_start(gain[:], gn.rearrange("(b p) o -> p (b o)", p=P))
+        w_w = keep.tile([P, 2 * N], U8, name="w_w", align_bytes=64)
+        nc.gpsimd.dma_start(w_w[:].bitcast(I32), w1_words[0].bitcast(I32))
+        for q in range(4):
+            nc.gpsimd.dma_start(w_sc[32 * q : 32 * q + 4, :].bitcast(I32), w1_scales[0, 4 * q : 4 * q + 4, :].bitcast(I32))
+        ident = keep.tile([P, P], F32, name="ident")
+        make_identity(nc, ident[:])
+
+        def gather(dst, table, lst, a, n):
+            nc.vector.tensor_copy(dst, table.indirect(lst[:, a // 16 : (a + n) // 16]))
+
+        def move_rows(plane, picked):
+            for r in range(4):
+                eng = nc.scalar if r % 2 else nc.sync
+                eng.dma_start(plane[r:P:32, :].bitcast(I32), picked[8 * r : P : 32, :].bitcast(I32))
+
+        d_g = {}
+        x_g = [keep.tile([P, S], U32, name=f"x_g{u}", align_bytes=64) for u in range(3)]
+        ds = [[keep.tile([P, SPARE], F32, name=f"ds{b}{s}") for s in range(2)] for b in range(4)]
+        zt_ps = [psum.tile([P, H], F32, name=f"zt_ps{c}") for c in range(2)]
+        zt = [keep.tile([P, H], BF16, name=f"zt{c}", align_bytes=64) for c in range(2)]
+
+        def first_product(b, j0, nj):
+            h, m0 = b // 2, (b % 2) * P
+            plane = plane1 if h else plane0
+            acc = psum.tile([P, S], F32, name="acc", tag="acc", bufs=4)
+            for u in range(3):
+                nc.tensor.matmul_mx(
+                    out=acc[:, 0:nj],
+                    lhsT=d_g[h][u][:, m0 : m0 + P].bitcast(FP8X4),
+                    lhsT_scale=plane[:, u * HALF + m0 : u * HALF + m0 + P],
+                    rhs=x_g[u][:, j0 : j0 + nj].bitcast(FP8X4),
+                    rhs_scale=plane0[:, 3 * HALF + u * S + j0 : 3 * HALF + u * S + j0 + nj],
+                    start=(u == 0),
+                    stop=(u == 2),
+                )
+            hg = keep.tile([P, nj], F32, name=f"hg{b}_{j0}")
+            if b == 0:
+                nc.scalar.activation(hg[:], acc[:, 0:nj], COPY, scale=gain[:, b : b + 1])
+            else:
+                nc.vector.tensor_scalar(hg[:], acc[:, 0:nj], gain[:, b : b + 1], None, ALU.mult)
+            for s, (lst, scale) in enumerate(((l_n1, 0.0625), (l_n2, -0.0625))):
+                nc.scalar.activation(ds[b][s][:].indirect(lst[:, j0 // 16 : (j0 + nj) // 16]), hg[:], COPY, scale=scale)
+
+        def turn(b):
+            for c in range(2):
+                for s in range(2):
+                    nc.tensor.matmul(
+                        zt_ps[c][:, b * P : (b + 1) * P],
+                        lhsT=ds[b][s][:, c * P : (c + 1) * P],
+                        rhs=ident[:],
+                        start=(s == 0),
+                        stop=(s == 1),
+                        is_transpose=True,
+                    )
+            for c in range(2):
+                dst = zt[c][:].rearrange("j (u p e) -> j u p e", u=2, e=2)[:, :, 32 * b : 32 * (b + 1), :]
+                src = zt_ps[c][:, b * P : (b + 1) * P].rearrange("j (p u e) -> j u p e", u=2, e=2)
+                if b == 3 and c == 1:
+                    nc.scalar.copy(dst, src)
+                else:
+                    nc.vector.tensor_copy(dst, src)
+
+        picked0 = keep.tile([P, 3 * HALF + 3 * S], U8, name="picked0", tag="picked", align_bytes=64)
+        for u in range(3):
+            gather(picked0[:, u * HALF : (u + 1) * HALF], d_sc[:], d_lists[u], 0, HALF)
+        for u in range(3):
+            gather(picked0[:, 3 * HALF + u * S : 3 * HALF + (u + 1) * S], x_sc[:], x_lists[u], 0, S)
+        move_rows(plane0, picked0)
+        d_g[0] = [keep.tile([P, HALF], U32, name=f"d_g0{u}", tag=f"d_g{u}", align_bytes=64) for u in range(3)]
+        for u in range(3):
+            gather(d_g[0][u][:], d_w[:].bitcast(U32), d_lists[u], 0, HALF)
+        for u in range(3):
+            gather(x_g[u][:, 0:P], x_w[:].bitcast(U32), x_lists[u], 0, P)
+        first_product(0, 0, P)
+        for u in range(3):
+            gather(x_g[u][:, P:S], x_w[:].bitcast(U32), x_lists[u], P, P)
+        first_product(0, P, P)
+        first_product(1, 0, S)
+        picked1 = keep.tile([P, 3 * HALF], U8, name="picked1", tag="picked", align_bytes=64)
+        for u in range(3):
+            gather(picked1[:, u * HALF : (u + 1) * HALF], d_sc[:], d_lists[u], HALF, HALF)
+        move_rows(plane1, picked1)
+        d_g[1] = [keep.tile([P, HALF], U32, name=f"d_g1{u}", tag=f"d_g{u}", align_bytes=64) for u in range(3)]
+        for u in range(3):
+            gather(d_g[1][u][:], d_w[:].bitcast(U32), d_lists[u], HALF, HALF)
+        first_product(2, 0, S)
+        first_product(3, 0, S)
+        for b in range(4):
+            turn(b)
+
+        grouped = keep.tile([P, 4 * S], BF16, name="grouped", align_bytes=64)
+        for c in range(2):
+            zq_ps = psum.tile([P, 2, P], F32, name=f"zq_ps{c}")
+            words = zt[c][:].bitcast(F32)
+            for u in range(2):
+                nc.tensor.transpose(zq_ps[:, u, :], words[:, u * P : (u + 1) * P], ident[:])
+            dst = grouped[:].bitcast(F32)[:, 2 * P * c : 2 * P * (c + 1)].rearrange("p (j u) -> p j u", u=2)
+            src = zq_ps[:].rearrange("p u j -> p j u")
+            if c == 1:
+                nc.scalar.copy(dst, src)
+            else:
+                nc.vector.tensor_copy(dst, src)
+        z_w = keep.tile([P, S], U32, name="z_w", align_bytes=64)
+        z_sc = keep.tile([P, S], U8, name="z_sc", align_bytes=64)
+        nc.vector.quantize_mx(out=z_w[:].bitcast(FP8X4), scales=z_sc[:], in_=grouped[:])
+
+        h2 = []
+        for a in range(4):
+            acc = psum.tile([P, S], F32, name="acc", tag="acc", bufs=4)
+            nc.tensor.matmul_mx(
+                out=acc[:],
+                lhsT=w_w[:, 2 * P * a : 2 * P * (a + 1)].bitcast(FP4X4),
+                lhsT_scale=w_sc[:, P * a : P * (a + 1)],
+                rhs=z_w[:].bitcast(FP8X4),
+                rhs_scale=z_sc[:],
+                start=True,
+                stop=True,
+            )
+            t = keep.tile([P, S], F32, name=f"h2_{a}")
+            nc.vector.tensor_copy(t[:], acc[:])
+            h2.append(t)
+
+        pairs = {}
+
+        def fetch(a):
+            pa = keep.tile([P, W], F32, name=f"pa{a}")
+            pb = keep.tile([P, W], F32, name=f"pb{a}")
+            nc.scalar.activation(pa[:], h2[a][:].indirect(l_n3[:]), COPY)
+            nc.scalar.activation(pb[:], h2[a][:].indirect(l_n4[:]), COPY)
+            total = keep.tile([P, W], F32, name=f"total{a}")
+            diff = keep.tile([P, W], F32, name=f"diff{a}")
+            nc.vector.tensor_tensor(total[:], pa[:], pb[:], ALU.add)
+            nc.vector.tensor_tensor(diff[:], pa[:], pb[:], ALU.subtract)
+            pairs[a] = (total, diff)
+
+        def put(a):
+            total, diff = pairs[a]
+            res = keep.tile([P, S], F32, name=f"res{a}")
+            nc.scalar.activation(res[:].indirect(l_n3[:]), total[:], COPY, scale=0.75)
+            nc.scalar.activation(res[:].indirect(l_n4[:]), diff[:], COPY)
+            nc.sync.dma_start(out[a * P : (a + 1) * P, :], res[:])
+
+        fetch(0)
+        for a in range(1, 4):
+            fetch(a)
+            put(a - 1)
+        put(3)

@@ -35,74 +35,73 @@ def tile_picked_mtthznsndsubhaar_none_p_kernel(
             nc.sync.dma_start(t[:], src)
             return t
 
-        d_sc = keep.tile([P, G], U8, name="d_sc", align_bytes=64)
-        x_sc = keep.tile([P, T], U8, name="x_sc", align_bytes=64)
+        d_sc = keep.tile([P, G], U8, name="d_sc", tag="d_sc", align_bytes=64)
+        x_sc = keep.tile([P, T], U8, name="x_sc", tag="x_sc", align_bytes=64)
         plane0 = keep.tile([P, 3 * HALF + 3 * S], U8, name="plane0", align_bytes=64)
         plane1 = keep.tile([P, 3 * HALF], U8, name="plane1", align_bytes=64)
-        w_sc = keep.tile([P, N], U8, name="w_sc", align_bytes=64)
-        nc.vector.memset(w_sc[:].bitcast(I32), 0)
         nc.vector.memset(plane0[:].bitcast(I32), 0)
         nc.vector.memset(plane1[:].bitcast(I32), 0)
 
         d_w = keep.tile([P, G], I32, name="d_w", align_bytes=64)
         x_w = keep.tile([P, T], I32, name="x_w", align_bytes=64)
+        def load_scales(dst, src):
+            rows = src[0].bitcast(I32).unsqueeze(1)
+            nc.sync.dma_start(dst[:].bitcast(I32), rows.to_broadcast([16, 8, rows.shape[-1]]))
+
+        load_scales(x_sc, x_scales)
+        l_hz = load_list("l_hz", hz)
+        l_offs = load_list("l_offs", offs)
         l_k1 = load_list("l_k1", k1)
-        nc.sync.dma_start(d_sc[:].bitcast(I32), d_scales[0].bitcast(I32).unsqueeze(1).to_broadcast([16, 8, G // 4]))
+        load_scales(d_sc, d_scales)
         l_k2 = load_list("l_k2", k2)
         l_k3 = load_list("l_k3", k3)
-        nc.sync.dma_start(x_sc[:].bitcast(I32), x_scales[0].bitcast(I32).unsqueeze(1).to_broadcast([16, 8, T // 4]))
-        l_offs = load_list("l_offs", offs)
-        l_two = load_list("l_two", two)
-        l_hz = load_list("l_hz", hz)
         nc.sync.dma_start(d_w[:], d_words[0].rearrange("p n t -> p (n t)").bitcast(I32))
-        nc.sync.dma_start(x_w[:], x_words[0].rearrange("p n t -> p (n t)").bitcast(I32))
+        l_two = load_list("l_two", two)
         l_n1 = load_list("l_n1", n1)
         l_n2 = load_list("l_n2", n2)
+        nc.sync.dma_start(x_w[:], x_words[0].rearrange("p n t -> p (n t)").bitcast(I32))
+        gain = keep.tile([P, 4], F32, name="gain")
+        with nc.allow_non_contiguous_dma(reason="one gain a partition"):
+            nc.sync.dma_start(gain[:], gn.rearrange("(b p) o -> p (b o)", p=P))
         l_n3 = load_list("l_n3", n3)
         l_n4 = load_list("l_n4", n4)
         d_lists = [l_k1, l_k2, l_k3]
         x_lists = [l_offs, l_two, l_hz]
 
-        gain = keep.tile([P, 4], F32, name="gain")
-        with nc.allow_non_contiguous_dma(reason="one gain a partition"):
-            nc.gpsimd.dma_start(gain[:], gn.rearrange("(b p) o -> p (b o)", p=P))
-        w_w = keep.tile([P, 2 * N], U8, name="w_w", align_bytes=64)
-        nc.gpsimd.dma_start(w_w[:].bitcast(I32), w1_words[0].bitcast(I32))
-        for q in range(4):
-            nc.gpsimd.dma_start(w_sc[32 * q : 32 * q + 4, :].bitcast(I32), w1_scales[0, 4 * q : 4 * q + 4, :].bitcast(I32))
         ident = keep.tile([P, P], F32, name="ident")
         make_identity(nc, ident[:])
 
         def gather(dst, table, lst, a, n):
             nc.vector.tensor_copy(dst, table.indirect(lst[:, a // 16 : (a + n) // 16]))
 
-        def move_rows(plane, picked):
+        def move_rows(plane, picked, queues):
             for r in range(4):
-                eng = nc.scalar if r % 2 else nc.sync
+                eng = queues[r % len(queues)]
                 eng.dma_start(plane[r:P:32, :].bitcast(I32), picked[8 * r : P : 32, :].bitcast(I32))
 
         d_g = {}
         x_g = [keep.tile([P, S], U32, name=f"x_g{u}", align_bytes=64) for u in range(3)]
+        x_plane = [plane0[:, 3 * HALF + u * S : 3 * HALF + (u + 1) * S] for u in range(3)]
         ds = [[keep.tile([P, SPARE], F32, name=f"ds{b}{s}") for s in range(2)] for b in range(4)]
-        zt_ps = [psum.tile([P, H], F32, name=f"zt_ps{c}") for c in range(2)]
+        zt_ps = []
         zt = [keep.tile([P, H], BF16, name=f"zt{c}", align_bytes=64) for c in range(2)]
 
         def first_product(b, j0, nj):
             h, m0 = b // 2, (b % 2) * P
             plane = plane1 if h else plane0
-            acc = psum.tile([P, S], F32, name="acc", tag="acc", bufs=4)
+            acc = psum.tile([P, S], F32, name=f"acc{b}_{j0}", tag=f"bank{b}_{j0}")
             for u in range(3):
                 nc.tensor.matmul_mx(
                     out=acc[:, 0:nj],
-                    lhsT=d_g[h][u][:, m0 : m0 + P].bitcast(FP8X4),
+                    lhsT=d_g[h][:, u, m0 : m0 + P].bitcast(FP8X4),
                     lhsT_scale=plane[:, u * HALF + m0 : u * HALF + m0 + P],
                     rhs=x_g[u][:, j0 : j0 + nj].bitcast(FP8X4),
-                    rhs_scale=plane0[:, 3 * HALF + u * S + j0 : 3 * HALF + u * S + j0 + nj],
+                    rhs_scale=x_plane[u][:, j0 : j0 + nj],
                     start=(u == 0),
                     stop=(u == 2),
                 )
             hg = keep.tile([P, nj], F32, name=f"hg{b}_{j0}")
-            if b == 0:
+            if b == 0 and j0 == 0:
                 nc.scalar.activation(hg[:], acc[:, 0:nj], COPY, scale=gain[:, b : b + 1])
             else:
                 nc.vector.tensor_scalar(hg[:], acc[:, 0:nj], gain[:, b : b + 1], None, ALU.mult)
@@ -110,8 +109,8 @@ def tile_picked_mtthznsndsubhaar_none_p_kernel(
                 nc.scalar.activation(ds[b][s][:].indirect(lst[:, j0 // 16 : (j0 + nj) // 16]), hg[:], COPY, scale=scale)
 
         def turn(b):
-            for c in range(2):
-                for s in range(2):
+            for s in range(2):
+                for c in range(2):
                     nc.tensor.matmul(
                         zt_ps[c][:, b * P : (b + 1) * P],
                         lhsT=ds[b][s][:, c * P : (c + 1) * P],
@@ -129,64 +128,77 @@ def tile_picked_mtthznsndsubhaar_none_p_kernel(
                     nc.vector.tensor_copy(dst, src)
 
         picked0 = keep.tile([P, 3 * HALF + 3 * S], U8, name="picked0", tag="picked", align_bytes=64)
+        for u in (2, 0):
+            gather(picked0[:, 3 * HALF + u * S : 3 * HALF + (u + 1) * S], x_sc[:], x_lists[u], 0, S)
         for u in range(3):
             gather(picked0[:, u * HALF : (u + 1) * HALF], d_sc[:], d_lists[u], 0, HALF)
+        gather(picked0[:, 3 * HALF + S : 3 * HALF + 2 * S], x_sc[:], l_two, 0, S)
+        move_rows(plane0, picked0, [nc.sync, nc.scalar])
+        d_g[0] = keep.tile([P, 3, HALF], U32, name="d_g0", tag="x_sc", align_bytes=64)
         for u in range(3):
-            gather(picked0[:, 3 * HALF + u * S : 3 * HALF + (u + 1) * S], x_sc[:], x_lists[u], 0, S)
-        move_rows(plane0, picked0)
-        d_g[0] = [keep.tile([P, HALF], U32, name=f"d_g0{u}", tag=f"d_g{u}", align_bytes=64) for u in range(3)]
-        for u in range(3):
-            gather(d_g[0][u][:], d_w[:].bitcast(U32), d_lists[u], 0, HALF)
-        for u in range(3):
-            gather(x_g[u][:, 0:P], x_w[:].bitcast(U32), x_lists[u], 0, P)
-        first_product(0, 0, P)
-        for u in range(3):
-            gather(x_g[u][:, P:S], x_w[:].bitcast(U32), x_lists[u], P, P)
-        first_product(0, P, P)
+            gather(d_g[0][:, u, :], d_w[:].bitcast(U32), d_lists[u], 0, HALF)
+        for j0 in (0, P):
+            for u in range(3):
+                gather(x_g[u][:, j0 : j0 + P], x_w[:].bitcast(U32), x_lists[u], j0, P)
+            first_product(0, j0, P)
         first_product(1, 0, S)
         picked1 = keep.tile([P, 3 * HALF], U8, name="picked1", tag="picked", align_bytes=64)
         for u in range(3):
             gather(picked1[:, u * HALF : (u + 1) * HALF], d_sc[:], d_lists[u], HALF, HALF)
-        move_rows(plane1, picked1)
-        d_g[1] = [keep.tile([P, HALF], U32, name=f"d_g1{u}", tag=f"d_g{u}", align_bytes=64) for u in range(3)]
+        move_rows(plane1, picked1, [nc.sync])
+        d_g[1] = keep.tile([P, 3, HALF], U32, name="d_g1", tag="x_sc", align_bytes=64)
         for u in range(3):
-            gather(d_g[1][u][:], d_w[:].bitcast(U32), d_lists[u], HALF, HALF)
+            gather(d_g[1][:, u, :], d_w[:].bitcast(U32), d_lists[u], HALF, HALF)
+        w_w = keep.tile([P, 2 * N], U8, name="w_w", tag="d_sc", align_bytes=64)
+        nc.sync.dma_start(w_w[:].bitcast(I32), w1_words[0].bitcast(I32))
+        w_sc = keep.tile([P, N], U8, name="w_sc", tag="picked", align_bytes=64)
+        nc.gpsimd.memset(w_sc[:].bitcast(I32), 0)
+        for q in range(4):
+            nc.sync.dma_start(w_sc[32 * q : 32 * q + 4, :].bitcast(I32), w1_scales[0, 4 * q : 4 * q + 4, :].bitcast(I32))
         first_product(2, 0, S)
         first_product(3, 0, S)
+        zt_ps.extend(psum.tile([P, H], F32, name=f"zt_ps{c}", tag=f"bank{3 - c}_0") for c in range(2))
         for b in range(4):
             turn(b)
 
-        grouped = keep.tile([P, 4 * S], BF16, name="grouped", align_bytes=64)
+        z_w = keep.tile([P, S], U32, name="z_w", align_bytes=64)
+        z_sc = keep.tile([P, S], U8, name="z_sc", align_bytes=64)
         for c in range(2):
             zq_ps = psum.tile([P, 2, P], F32, name=f"zq_ps{c}")
             words = zt[c][:].bitcast(F32)
             for u in range(2):
                 nc.tensor.transpose(zq_ps[:, u, :], words[:, u * P : (u + 1) * P], ident[:])
-            dst = grouped[:].bitcast(F32)[:, 2 * P * c : 2 * P * (c + 1)].rearrange("p (j u) -> p j u", u=2)
+            grouped = keep.tile([P, 4 * P], BF16, name=f"grouped{c}", align_bytes=64)
+            dst = grouped[:].bitcast(F32).rearrange("p (j u) -> p j u", u=2)
             src = zq_ps[:].rearrange("p u j -> p j u")
             if c == 1:
                 nc.scalar.copy(dst, src)
             else:
                 nc.vector.tensor_copy(dst, src)
-        z_w = keep.tile([P, S], U32, name="z_w", align_bytes=64)
-        z_sc = keep.tile([P, S], U8, name="z_sc", align_bytes=64)
-        nc.vector.quantize_mx(out=z_w[:].bitcast(FP8X4), scales=z_sc[:], in_=grouped[:])
+            cols = slice(c * P, (c + 1) * P)
+            nc.vector.quantize_mx(out=z_w[:, cols].bitcast(FP8X4), scales=z_sc[:, cols], in_=grouped[:])
 
-        h2 = []
-        for a in range(4):
-            acc = psum.tile([P, S], F32, name="acc", tag="acc", bufs=4)
+        def second_product(a, j0, nj, bank, on_scalar):
+            acc = psum.tile([P, S], F32, name=f"h2_ps{a}_{j0}", tag=bank)
             nc.tensor.matmul_mx(
-                out=acc[:],
+                out=acc[:, 0:nj],
                 lhsT=w_w[:, 2 * P * a : 2 * P * (a + 1)].bitcast(FP4X4),
                 lhsT_scale=w_sc[:, P * a : P * (a + 1)],
-                rhs=z_w[:].bitcast(FP8X4),
-                rhs_scale=z_sc[:],
+                rhs=z_w[:, j0 : j0 + nj].bitcast(FP8X4),
+                rhs_scale=z_sc[:, j0 : j0 + nj],
                 start=True,
                 stop=True,
             )
-            t = keep.tile([P, S], F32, name=f"h2_{a}")
-            nc.vector.tensor_copy(t[:], acc[:])
-            h2.append(t)
+            if on_scalar:
+                nc.scalar.copy(h2[a][:, j0 : j0 + nj], acc[:, 0:nj])
+            else:
+                nc.vector.tensor_copy(h2[a][:, j0 : j0 + nj], acc[:, 0:nj])
+
+        h2 = [keep.tile([P, S], F32, name=f"h2_{a}") for a in range(4)]
+        second_product(0, 0, P, "bank0_0", False)
+        second_product(0, P, P, f"bank0_{P}", True)
+        for a, bank in ((1, "bank1_0"), (2, "bank4"), (3, "bank2_0")):
+            second_product(a, 0, S, bank, False)
 
         pairs = {}
 

@@ -20,6 +20,7 @@ ALU = mybir.AluOpType
 P = 128
 HALF = H // 2
 SPARE = 2 * S
+D_SPLIT = 7 * G // 8
 
 
 def tile_picked_mtthznsndsubhaar_none_p_kernel(
@@ -28,6 +29,7 @@ def tile_picked_mtthznsndsubhaar_none_p_kernel(
     nc = tc.nc
     with ExitStack() as ctx:
         keep = ctx.enter_context(tc.tile_pool(name="keep", bufs=1))
+        turns = ctx.enter_context(tc.tile_pool(name="turns", bufs=1))
         psum = ctx.enter_context(tc.psum_pool(name="psum", bufs=1))
 
         def load_list(name, src):
@@ -36,11 +38,12 @@ def tile_picked_mtthznsndsubhaar_none_p_kernel(
             return t
 
         d_sc = keep.tile([P, G], U8, name="d_sc", tag="d_sc", align_bytes=64)
-        x_sc = keep.tile([P, T], U8, name="x_sc", tag="x_sc", align_bytes=64)
-        plane0 = keep.tile([P, 3 * HALF + 3 * S], U8, name="plane0", align_bytes=64)
-        plane1 = keep.tile([P, 3 * HALF], U8, name="plane1", align_bytes=64)
-        nc.vector.memset(plane0[:].bitcast(I32), 0)
-        nc.vector.memset(plane1[:].bitcast(I32), 0)
+        x_sc = turns.tile([P, T], U8, name="x_sc", offset=512, align_bytes=64)
+        plane_a = keep.tile([P, 3 * HALF + 3 * P], U8, name="plane_a", align_bytes=64)
+        plane_b = keep.tile([P, 3 * P], U8, name="plane_b", align_bytes=64)
+        plane_c = keep.tile([P, 3 * HALF], U8, name="plane_c", align_bytes=64)
+        for plane in (plane_a, plane_b, plane_c):
+            nc.vector.memset(plane[:].bitcast(I32), 0)
 
         d_w = keep.tile([P, G], I32, name="d_w", align_bytes=64)
         x_w = keep.tile([P, T], I32, name="x_w", align_bytes=64)
@@ -55,8 +58,10 @@ def tile_picked_mtthznsndsubhaar_none_p_kernel(
         load_scales(d_sc, d_scales)
         l_k2 = load_list("l_k2", k2)
         l_k3 = load_list("l_k3", k3)
-        nc.sync.dma_start(d_w[:], d_words[0].rearrange("p n t -> p (n t)").bitcast(I32))
+        d_src = d_words[0].rearrange("p n t -> p (n t)").bitcast(I32)
+        nc.sync.dma_start(d_w[:, 0:D_SPLIT], d_src[:, 0:D_SPLIT])
         l_two = load_list("l_two", two)
+        nc.sync.dma_start(d_w[:, D_SPLIT:G], d_src[:, D_SPLIT:G])
         l_n1 = load_list("l_n1", n1)
         l_n2 = load_list("l_n2", n2)
         nc.sync.dma_start(x_w[:], x_words[0].rearrange("p n t -> p (n t)").bitcast(I32))
@@ -80,28 +85,30 @@ def tile_picked_mtthznsndsubhaar_none_p_kernel(
                 eng.dma_start(plane[r:P:32, :].bitcast(I32), picked[8 * r : P : 32, :].bitcast(I32))
 
         d_g = {}
-        x_g = [keep.tile([P, S], U32, name=f"x_g{u}", align_bytes=64) for u in range(3)]
-        x_plane = [plane0[:, 3 * HALF + u * S : 3 * HALF + (u + 1) * S] for u in range(3)]
+        x_g = {}
+        d_plane = [plane_a, plane_c]
+        x_plane = [plane_a[:, 3 * HALF : 3 * HALF + 3 * P], plane_b[:]]
         ds = [[keep.tile([P, SPARE], F32, name=f"ds{b}{s}") for s in range(2)] for b in range(4)]
         zt_ps = []
         zt = [keep.tile([P, H], BF16, name=f"zt{c}", align_bytes=64) for c in range(2)]
 
-        def first_product(b, j0, nj):
+        def first_product(b, halves, on_scalar):
             h, m0 = b // 2, (b % 2) * P
-            plane = plane1 if h else plane0
+            j0, nj = halves[0] * P, len(halves) * P
             acc = psum.tile([P, S], F32, name=f"acc{b}_{j0}", tag=f"bank{b}_{j0}")
-            for u in range(3):
-                nc.tensor.matmul_mx(
-                    out=acc[:, 0:nj],
-                    lhsT=d_g[h][:, u, m0 : m0 + P].bitcast(FP8X4),
-                    lhsT_scale=plane[:, u * HALF + m0 : u * HALF + m0 + P],
-                    rhs=x_g[u][:, j0 : j0 + nj].bitcast(FP8X4),
-                    rhs_scale=x_plane[u][:, j0 : j0 + nj],
-                    start=(u == 0),
-                    stop=(u == 2),
-                )
+            for i, c in enumerate(halves):
+                for u in range(3):
+                    nc.tensor.matmul_mx(
+                        out=acc[:, i * P : (i + 1) * P],
+                        lhsT=d_g[h][:, u, m0 : m0 + P].bitcast(FP8X4),
+                        lhsT_scale=d_plane[h][:, u * HALF + m0 : u * HALF + m0 + P],
+                        rhs=x_g[c][:, u, :].bitcast(FP8X4),
+                        rhs_scale=x_plane[c][:, u * P : (u + 1) * P],
+                        start=(u == 0),
+                        stop=(u == 2),
+                    )
             hg = keep.tile([P, nj], F32, name=f"hg{b}_{j0}")
-            if b == 0 and j0 == 0:
+            if on_scalar:
                 nc.scalar.activation(hg[:], acc[:, 0:nj], COPY, scale=gain[:, b : b + 1])
             else:
                 nc.vector.tensor_scalar(hg[:], acc[:, 0:nj], gain[:, b : b + 1], None, ALU.mult)
@@ -127,26 +134,37 @@ def tile_picked_mtthznsndsubhaar_none_p_kernel(
                 else:
                     nc.vector.tensor_copy(dst, src)
 
-        picked0 = keep.tile([P, 3 * HALF + 3 * S], U8, name="picked0", tag="picked", align_bytes=64)
+        picked_a = keep.tile([P, 3 * HALF + 3 * P], U8, name="picked_a", tag="picked", align_bytes=64)
         for u in (2, 0):
-            gather(picked0[:, 3 * HALF + u * S : 3 * HALF + (u + 1) * S], x_sc[:], x_lists[u], 0, S)
+            gather(picked_a[:, 3 * HALF + u * P : 3 * HALF + (u + 1) * P], x_sc[:], x_lists[u], 0, P)
         for u in range(3):
-            gather(picked0[:, u * HALF : (u + 1) * HALF], d_sc[:], d_lists[u], 0, HALF)
-        gather(picked0[:, 3 * HALF + S : 3 * HALF + 2 * S], x_sc[:], l_two, 0, S)
-        move_rows(plane0, picked0, [nc.sync, nc.scalar])
-        d_g[0] = keep.tile([P, 3, HALF], U32, name="d_g0", tag="x_sc", align_bytes=64)
+            gather(picked_a[:, u * HALF : (u + 1) * HALF], d_sc[:], d_lists[u], 0, HALF)
+        gather(picked_a[:, 3 * HALF + P : 3 * HALF + 2 * P], x_sc[:], l_two, 0, P)
+        move_rows(plane_a, picked_a, [nc.sync])
+        d_g[0] = keep.tile([P, 3, HALF], U32, name="d_g0", tag="d_g", align_bytes=64)
         for u in range(3):
             gather(d_g[0][:, u, :], d_w[:].bitcast(U32), d_lists[u], 0, HALF)
-        for j0 in (0, P):
-            for u in range(3):
-                gather(x_g[u][:, j0 : j0 + P], x_w[:].bitcast(U32), x_lists[u], j0, P)
-            first_product(0, j0, P)
-        first_product(1, 0, S)
-        picked1 = keep.tile([P, 3 * HALF], U8, name="picked1", tag="picked", align_bytes=64)
+        x_g[0] = keep.tile([P, 3, P], U32, name="x_g0", align_bytes=64)
         for u in range(3):
-            gather(picked1[:, u * HALF : (u + 1) * HALF], d_sc[:], d_lists[u], HALF, HALF)
-        move_rows(plane1, picked1, [nc.sync])
-        d_g[1] = keep.tile([P, 3, HALF], U32, name="d_g1", tag="x_sc", align_bytes=64)
+            gather(x_g[0][:, u, :], x_w[:].bitcast(U32), x_lists[u], 0, P)
+        first_product(0, [0], True)
+        first_product(1, [0], True)
+
+        picked_b = keep.tile([P, 3 * P], U8, name="picked_b", tag="picked", align_bytes=64)
+        for u in range(3):
+            gather(picked_b[:, u * P : (u + 1) * P], x_sc[:], x_lists[u], P, P)
+        move_rows(plane_b, picked_b, [nc.sync])
+        x_g[1] = turns.tile([P, 3, P], U32, name="x_g1", offset=768, align_bytes=64)
+        for u in range(3):
+            gather(x_g[1][:, u, :], x_w[:].bitcast(U32), x_lists[u], P, P)
+        picked_c = turns.tile([P, 3 * HALF], U8, name="picked_c", offset=0, align_bytes=64)
+        for u in range(3):
+            gather(picked_c[:, u * HALF : (u + 1) * HALF], d_sc[:], d_lists[u], HALF, HALF)
+        move_rows(plane_c, picked_c, [nc.sync])
+        first_product(0, [1], False)
+        first_product(1, [1], False)
+
+        d_g[1] = keep.tile([P, 3, HALF], U32, name="d_g1", tag="d_g", align_bytes=64)
         for u in range(3):
             gather(d_g[1][:, u, :], d_w[:].bitcast(U32), d_lists[u], HALF, HALF)
         w_w = keep.tile([P, 2 * N], U8, name="w_w", tag="d_sc", align_bytes=64)
@@ -155,8 +173,8 @@ def tile_picked_mtthznsndsubhaar_none_p_kernel(
         nc.gpsimd.memset(w_sc[:].bitcast(I32), 0)
         for q in range(4):
             nc.sync.dma_start(w_sc[32 * q : 32 * q + 4, :].bitcast(I32), w1_scales[0, 4 * q : 4 * q + 4, :].bitcast(I32))
-        first_product(2, 0, S)
-        first_product(3, 0, S)
+        first_product(2, [0, 1], False)
+        first_product(3, [0, 1], False)
         zt_ps.extend(psum.tile([P, H], F32, name=f"zt_ps{c}", tag=f"bank{3 - c}_0") for c in range(2))
         for b in range(4):
             turn(b)
@@ -197,7 +215,7 @@ def tile_picked_mtthznsndsubhaar_none_p_kernel(
         h2 = [keep.tile([P, S], F32, name=f"h2_{a}") for a in range(4)]
         second_product(0, 0, P, "bank0_0", False)
         second_product(0, P, P, f"bank0_{P}", True)
-        for a, bank in ((1, "bank1_0"), (2, "bank4"), (3, "bank2_0")):
+        for a, bank in ((1, "bank1_0"), (2, f"bank1_{P}"), (3, "bank2_0")):
             second_product(a, 0, S, bank, False)
 
         pairs = {}

from contextlib import ExitStack

import concourse.mybir as mybir
from concourse.masks import make_identity

K, T, S, N, G, H, W = 512, 1024, 256, 512, 2048, 512, 128
FLOPS = 2 * K * H * S * 3 + 2 * H * N * S

F32 = mybir.dt.float32
BF16 = mybir.dt.bfloat16
I32 = mybir.dt.int32
U32 = mybir.dt.uint32
U16 = mybir.dt.uint16
U8 = mybir.dt.uint8
FP8X4 = mybir.dt.float8_e4m3fn_x4
FP4X4 = mybir.dt.float4_e2m1fn_x4
COPY = mybir.ActivationFunctionType.Copy
ALU = mybir.AluOpType

P = 128
HALF = H // 2
SPARE = 2 * S
D_SPLIT = 7 * G // 8


def tile_picked_mtthznsndsubhaar_none_p_kernel(
    tc, x_words, x_scales, d_words, d_scales, gn, w1_words, w1_scales, offs, k1, two, k2, hz, k3, n1, n2, n3, n4, out
):
    nc = tc.nc
    with ExitStack() as ctx:
        keep = ctx.enter_context(tc.tile_pool(name="keep", bufs=1))
        turns = ctx.enter_context(tc.tile_pool(name="turns", bufs=1))
        psum = ctx.enter_context(tc.psum_pool(name="psum", bufs=1))

        def load_list(name, src):
            t = keep.tile(list(src.shape), U16, name=name)
            nc.sync.dma_start(t[:], src)
            return t

        d_sc = keep.tile([P, G], U8, name="d_sc", tag="d_sc", align_bytes=64)
        x_sc = turns.tile([P, T], U8, name="x_sc", offset=512, align_bytes=64)
        plane_a = keep.tile([P, 3 * HALF + 3 * P], U8, name="plane_a", align_bytes=64)
        plane_b = keep.tile([P, 3 * P], U8, name="plane_b", align_bytes=64)
        plane_c = keep.tile([P, 3 * HALF], U8, name="plane_c", align_bytes=64)
        for plane in (plane_a, plane_b, plane_c):
            nc.vector.memset(plane[:].bitcast(I32), 0)

        d_w = keep.tile([P, G], I32, name="d_w", align_bytes=64)
        x_w = keep.tile([P, T], I32, name="x_w", align_bytes=64)
        def load_scales(dst, src):
            rows = src[0].bitcast(I32).unsqueeze(1)
            nc.sync.dma_start(dst[:].bitcast(I32), rows.to_broadcast([16, 8, rows.shape[-1]]))

        load_scales(x_sc, x_scales)
        l_hz = load_list("l_hz", hz)
        l_offs = load_list("l_offs", offs)
        l_k1 = load_list("l_k1", k1)
        load_scales(d_sc, d_scales)
        l_k2 = load_list("l_k2", k2)
        l_k3 = load_list("l_k3", k3)
        d_src = d_words[0].rearrange("p n t -> p (n t)").bitcast(I32)
        nc.sync.dma_start(d_w[:, 0:D_SPLIT], d_src[:, 0:D_SPLIT])
        l_two = load_list("l_two", two)
        nc.sync.dma_start(d_w[:, D_SPLIT:G], d_src[:, D_SPLIT:G])
        l_n1 = load_list("l_n1", n1)
        l_n2 = load_list("l_n2", n2)
        nc.sync.dma_start(x_w[:], x_words[0].rearrange("p n t -> p (n t)").bitcast(I32))
        gain = keep.tile([P, 4], F32, name="gain")
        with nc.allow_non_contiguous_dma(reason="one gain a partition"):
            nc.sync.dma_start(gain[:], gn.rearrange("(b p) o -> p (b o)", p=P))
        l_n3 = load_list("l_n3", n3)
        l_n4 = load_list("l_n4", n4)
        d_lists = [l_k1, l_k2, l_k3]
        x_lists = [l_offs, l_two, l_hz]

        ident = keep.tile([P, P], F32, name="ident")
        make_identity(nc, ident[:])

        def gather(dst, table, lst, a, n):
            nc.vector.tensor_copy(dst, table.indirect(lst[:, a // 16 : (a + n) // 16]))

        def move_rows(plane, picked, queues):
            for r in range(4):
                eng = queues[r % len(queues)]
                eng.dma_start(plane[r:P:32, :].bitcast(I32), picked[8 * r : P : 32, :].bitcast(I32))

        d_g = {}
        x_g = {}
        d_plane = [plane_a, plane_c]
        x_plane = [plane_a[:, 3 * HALF : 3 * HALF + 3 * P], plane_b[:]]
        ds = [[keep.tile([P, SPARE], F32, name=f"ds{b}{s}") for s in range(2)] for b in range(4)]
        zt_ps = []
        zt = [keep.tile([P, H], BF16, name=f"zt{c}", align_bytes=64) for c in range(2)]

        def first_product(b, halves, on_scalar):
            h, m0 = b // 2, (b % 2) * P
            j0, nj = halves[0] * P, len(halves) * P
            acc = psum.tile([P, S], F32, name=f"acc{b}_{j0}", tag=f"bank{b}_{j0}")
            for i, c in enumerate(halves):
                for u in range(3):
                    nc.tensor.matmul_mx(
                        out=acc[:, i * P : (i + 1) * P],
                        lhsT=d_g[h][:, u, m0 : m0 + P].bitcast(FP8X4),
                        lhsT_scale=d_plane[h][:, u * HALF + m0 : u * HALF + m0 + P],
                        rhs=x_g[c][:, u, :].bitcast(FP8X4),
                        rhs_scale=x_plane[c][:, u * P : (u + 1) * P],
                        start=(u == 0),
                        stop=(u == 2),
                    )
            hg = keep.tile([P, nj], F32, name=f"hg{b}_{j0}")
            if on_scalar:
                nc.scalar.activation(hg[:], acc[:, 0:nj], COPY, scale=gain[:, b : b + 1])
            else:
                nc.vector.tensor_scalar(hg[:], acc[:, 0:nj], gain[:, b : b + 1], None, ALU.mult)
            for s, (lst, scale) in enumerate(((l_n1, 0.0625), (l_n2, -0.0625))):
                nc.scalar.activation(ds[b][s][:].indirect(lst[:, j0 // 16 : (j0 + nj) // 16]), hg[:], COPY, scale=scale)

        def turn(b):
            for s in range(2):
                for c in range(2):
                    nc.tensor.matmul(
                        zt_ps[c][:, b * P : (b + 1) * P],
                        lhsT=ds[b][s][:, c * P : (c + 1) * P],
                        rhs=ident[:],
                        start=(s == 0),
                        stop=(s == 1),
                        is_transpose=True,
                    )
            for c in range(2):
                dst = zt[c][:].rearrange("j (u p e) -> j u p e", u=2, e=2)[:, :, 32 * b : 32 * (b + 1), :]
                src = zt_ps[c][:, b * P : (b + 1) * P].rearrange("j (p u e) -> j u p e", u=2, e=2)
                if b == 3 and c == 1:
                    nc.scalar.copy(dst, src)
                else:
                    nc.vector.tensor_copy(dst, src)

        picked_a = keep.tile([P, 3 * HALF + 3 * P], U8, name="picked_a", tag="picked", align_bytes=64)
        for u in (2, 0):
            gather(picked_a[:, 3 * HALF + u * P : 3 * HALF + (u + 1) * P], x_sc[:], x_lists[u], 0, P)
        for u in range(3):
            gather(picked_a[:, u * HALF : (u + 1) * HALF], d_sc[:], d_lists[u], 0, HALF)
        gather(picked_a[:, 3 * HALF + P : 3 * HALF + 2 * P], x_sc[:], l_two, 0, P)
        move_rows(plane_a, picked_a, [nc.sync])
        d_g[0] = keep.tile([P, 3, HALF], U32, name="d_g0", tag="d_g", align_bytes=64)
        for u in range(3):
            gather(d_g[0][:, u, :], d_w[:].bitcast(U32), d_lists[u], 0, HALF)
        x_g[0] = keep.tile([P, 3, P], U32, name="x_g0", align_bytes=64)
        for u in range(3):
            gather(x_g[0][:, u, :], x_w[:].bitcast(U32), x_lists[u], 0, P)
        first_product(0, [0], True)
        first_product(1, [0], True)

        picked_b = keep.tile([P, 3 * P], U8, name="picked_b", tag="picked", align_bytes=64)
        for u in range(3):
            gather(picked_b[:, u * P : (u + 1) * P], x_sc[:], x_lists[u], P, P)
        move_rows(plane_b, picked_b, [nc.sync])
        x_g[1] = turns.tile([P, 3, P], U32, name="x_g1", offset=768, align_bytes=64)
        for u in range(3):
            gather(x_g[1][:, u, :], x_w[:].bitcast(U32), x_lists[u], P, P)
        picked_c = turns.tile([P, 3 * HALF], U8, name="picked_c", offset=0, align_bytes=64)
        for u in range(3):
            gather(picked_c[:, u * HALF : (u + 1) * HALF], d_sc[:], d_lists[u], HALF, HALF)
        move_rows(plane_c, picked_c, [nc.sync])
        first_product(0, [1], False)
        first_product(1, [1], False)

        d_g[1] = keep.tile([P, 3, HALF], U32, name="d_g1", tag="d_g", align_bytes=64)
        for u in range(3):
            gather(d_g[1][:, u, :], d_w[:].bitcast(U32), d_lists[u], HALF, HALF)
        w_w = keep.tile([P, 2 * N], U8, name="w_w", tag="d_sc", align_bytes=64)
        nc.sync.dma_start(w_w[:].bitcast(I32), w1_words[0].bitcast(I32))
        w_sc = keep.tile([P, N], U8, name="w_sc", tag="picked", align_bytes=64)
        nc.gpsimd.memset(w_sc[:].bitcast(I32), 0)
        for q in range(4):
            nc.sync.dma_start(w_sc[32 * q : 32 * q + 4, :].bitcast(I32), w1_scales[0, 4 * q : 4 * q + 4, :].bitcast(I32))
        first_product(2, [0, 1], False)
        first_product(3, [0, 1], False)
        zt_ps.extend(psum.tile([P, H], F32, name=f"zt_ps{c}", tag=f"bank{3 - c}_0") for c in range(2))
        for b in range(4):
            turn(b)

        z_w = keep.tile([P, S], U32, name="z_w", align_bytes=64)
        z_sc = keep.tile([P, S], U8, name="z_sc", align_bytes=64)
        for c in range(2):
            zq_ps = psum.tile([P, 2, P], F32, name=f"zq_ps{c}")
            words = zt[c][:].bitcast(F32)
            for u in range(2):
                nc.tensor.transpose(zq_ps[:, u, :], words[:, u * P : (u + 1) * P], ident[:])
            grouped = keep.tile([P, 4 * P], BF16, name=f"grouped{c}", align_bytes=64)
            dst = grouped[:].bitcast(F32).rearrange("p (j u) -> p j u", u=2)
            src = zq_ps[:].rearrange("p u j -> p j u")
            if c == 1:
                nc.scalar.copy(dst, src)
            else:
                nc.vector.tensor_copy(dst, src)
            cols = slice(c * P, (c + 1) * P)
            nc.vector.quantize_mx(out=z_w[:, cols].bitcast(FP8X4), scales=z_sc[:, cols], in_=grouped[:])

        def second_product(a, j0, nj, bank, on_scalar):
            acc = psum.tile([P, S], F32, name=f"h2_ps{a}_{j0}", tag=bank)
            nc.tensor.matmul_mx(
                out=acc[:, 0:nj],
                lhsT=w_w[:, 2 * P * a : 2 * P * (a + 1)].bitcast(FP4X4),
                lhsT_scale=w_sc[:, P * a : P * (a + 1)],
                rhs=z_w[:, j0 : j0 + nj].bitcast(FP8X4),
                rhs_scale=z_sc[:, j0 : j0 + nj],
                start=True,
                stop=True,
            )
            if on_scalar:
                nc.scalar.copy(h2[a][:, j0 : j0 + nj], acc[:, 0:nj])
            else:
                nc.vector.tensor_copy(h2[a][:, j0 : j0 + nj], acc[:, 0:nj])

        h2 = [keep.tile([P, S], F32, name=f"h2_{a}") for a in range(4)]
        second_product(0, 0, P, "bank0_0", False)
        second_product(0, P, P, f"bank0_{P}", True)
        for a, bank in ((1, "bank1_0"), (2, f"bank1_{P}"), (3, "bank2_0")):
            second_product(a, 0, S, bank, False)

        pairs = {}

        def fetch(a):
            pa = keep.tile([P, W], F32, name=f"pa{a}")
            pb = keep.tile([P, W], F32, name=f"pb{a}")
            nc.scalar.activation(pa[:], h2[a][:].indirect(l_n3[:]), COPY)
            nc.scalar.activation(pb[:], h2[a][:].indirect(l_n4[:]), COPY)
            total = keep.tile([P, W], F32, name=f"total{a}")
            diff = keep.tile([P, W], F32, name=f"diff{a}")
            nc.vector.tensor_tensor(total[:], pa[:], pb[:], ALU.add)
            nc.vector.tensor_tensor(diff[:], pa[:], pb[:], ALU.subtract)
            pairs[a] = (total, diff)

        def put(a):
            total, diff = pairs[a]
            res = keep.tile([P, S], F32, name=f"res{a}")
            nc.scalar.activation(res[:].indirect(l_n3[:]), total[:], COPY, scale=0.75)
            nc.scalar.activation(res[:].indirect(l_n4[:]), diff[:], COPY)
            nc.sync.dma_start(out[a * P : (a + 1) * P, :], res[:])

        fetch(0)
        for a in range(1, 4):
            fetch(a)
            put(a - 1)
        put(3)
